import numpy as np
import ml_dtypes


def mxq(x, axis, fmt="e4m3"):
    dtype, down = {"e4m3": (ml_dtypes.float8_e4m3fn, 7), "e5m2": (ml_dtypes.float8_e5m2, 14)}[fmt]
    v = np.moveaxis(np.asarray(x, np.float32).astype(ml_dtypes.bfloat16).astype(np.float64), axis, -1)
    blocks = v.reshape(v.shape[:-1] + (-1, 32))
    amax = np.abs(blocks).max(-1, keepdims=True)
    byte = np.maximum(np.where(amax > 0, np.frexp(amax)[1] - 1 + 127, 0) - down, 1)
    scale = np.exp2(byte - 127.0)
    codes = (blocks / scale).astype(np.float32).astype(dtype).astype(np.float64)
    return np.moveaxis((codes * scale).reshape(v.shape), -1, axis)


WIDE = False


def mx_kscale(k):
    if not WIDE:
        return np.ones(k)
    levels = np.array([10, -10, 5, -5, 0])
    if k % 512:
        return np.exp2(np.random.permutation(np.resize(levels, k // 32))).repeat(32)
    a = np.empty((k // 512, 16))
    for p in range(k // 512):
        a[p, :8] = np.random.permutation(np.resize(levels, 8))
        for g in range(8):
            far = levels[np.abs(levels - a[p, g]) >= 10]
            a[p, g + 8] = far[np.random.randint(len(far))]
    return np.exp2(a.ravel()).repeat(32)


def f64(x):
    return np.asarray(x).astype(np.float64)


def striped(idx):
    return np.tile(idx.reshape(-1, 16).T, (8, 1)).astype(np.uint16)


def unstriped(offs):
    return offs[:16].T.reshape(-1).astype(np.int64)


E2M1 = np.array([0.0, 0.5, 1.0, 1.5, 2.0, 3.0, 4.0, 6.0, -0.0, -0.5, -1.0, -1.5, -2.0, -3.0, -4.0, -6.0])


def pack_weight(w, fmt):
    k, n = w.shape
    w = f64(np.asarray(w, np.float32).astype(ml_dtypes.bfloat16)).reshape(k // 32, 32, n)
    amax = np.abs(w).max(1)
    if fmt == "e4m3":
        byte = np.frexp(amax)[1] - 1 + 127 - 7
    else:
        mant, ex = np.frexp(amax / 6.0)
        byte = np.where(mant > 0.5, ex, ex - 1) + 127
    byte = np.clip(np.where(amax > 0, byte, 1), 1, 254)
    scaled = (w * np.exp2(127.0 - byte)[:, None, :]).reshape(k, n).astype(np.float32)
    by_word = np.ascontiguousarray(scaled.reshape(k // 512, 128, 4, n).transpose(0, 1, 3, 2))
    if fmt == "e4m3":
        words = by_word.astype(ml_dtypes.float8_e4m3fn).view(np.uint8)
    else:
        c = by_word.astype(ml_dtypes.float4_e2m1fn).view(np.uint8) & 0xF
        words = (c[..., 0::2] | (c[..., 1::2] << 4)).reshape(k // 512, 128, 2 * n)
    return np.ascontiguousarray(words), np.ascontiguousarray(byte.astype(np.uint8).reshape(k // 512, 16, n))


def unpack_weight(words, scales, fmt):
    g, _, n = scales.shape
    words = np.ascontiguousarray(words).reshape(g, 128, n, -1)
    if fmt == "e4m3":
        vals = words.view(ml_dtypes.float8_e4m3fn).astype(np.float64)
    else:
        nib = np.empty((g, 128, n, 4), np.uint8)
        nib[..., 0::2] = words & 0xF
        nib[..., 1::2] = words >> 4
        vals = E2M1[nib]
    vals = vals * np.repeat(np.exp2(scales.astype(np.float64) - 127.0), 8, axis=1)[..., None]
    return vals.transpose(0, 1, 3, 2).reshape(g * 512, n)


def gelu(v):
    return 0.5 * v * (1.0 + np.tanh(np.sqrt(2.0 / np.pi) * (v + 0.044715 * v**3)))


K, H, T, S, T2, P, T3, S2 = 1536, 1024, 2048, 512, 1024, 512, 2048, 1024


def setup_inputs():
    n = np.random.standard_normal
    s = mx_kscale(K)[:, None]
    u = mx_kscale(H)[:, None]
    tab_words, tab_scales = pack_weight(n((K, T)) * s, "e4m3")
    tab2_words, tab2_scales = pack_weight(n((H, T3)) / np.sqrt(H) / u, "e4m3")
    q4_words, q4_scales = pack_weight(0.8 * n((H, P)) * u, "e2m1")
    return {
        "tab_words": tab_words, "tab_scales": tab_scales,
        "offs": striped(np.random.permutation(T)[:S]),
        "tab2_words": tab2_words, "tab2_scales": tab2_scales,
        "offs2": striped(np.random.permutation(T3)[:S2]),
        "offs3": striped(np.random.permutation(T2)[:S]),
        "offs4": striped(np.random.permutation(T2)[:P]),
        "w1": (n((K, H)) / np.sqrt(K) / s * u.T).astype(np.float32),
        "b1": (0.6 * n(H) * u[:, 0]).astype(np.float32),
        "page0": (n((H, T2)) * u).astype(np.float32),
        "wgs": np.exp(0.3 * n((128, S))).astype(np.float32),
        "cov": np.random.uniform(0.4, 1.6, (H, P)).astype(np.float32),
        "q4_words": q4_words, "q4_scales": q4_scales,
        "cand": np.exp(0.3 * n(S2)).astype(np.float32),
    }


def reference(tab_words, tab_scales, offs, tab2_words, tab2_scales, offs2, offs3, offs4,
              w1, b1, page0, wgs, cov, q4_words, q4_scales, cand):
    v = unpack_weight(tab_words, tab_scales, "e4m3")[:, unstriped(offs)]
    v2 = unpack_weight(tab2_words, tab2_scales, "e4m3")[:, unstriped(offs2)]
    q4 = unpack_weight(q4_words, q4_scales, "e2m1")
    h = (mxq(f64(w1), 0, "e4m3").T @ v) + f64(b1)[:, None]
    page = f64(page0).copy()
    page[:, unstriped(offs3)] = np.tile(f64(wgs), (H // 128, 1)) * h
    x = page[:, unstriped(offs4)] * f64(cov)
    xq = mxq(x, 0, "e4m3")
    e = v2.T @ xq + v2.T @ q4
    return np.tanh(f64(cand)[:, None] * e)

@@ -1,0 +1,279 @@
+from contextlib import ExitStack
+
+import concourse.mybir as mybir
+from concourse.masks import make_identity
+
+K, H, T, S, T2, J, T3, S2 = 1536, 1024, 2048, 512, 1024, 512, 2048, 1024
+FLOPS = 2 * K * H * S + 2 * 2 * H * S2 * J
+
+F32 = mybir.dt.float32
+BF16 = mybir.dt.bfloat16
+I32 = mybir.dt.int32
+U32 = mybir.dt.uint32
+U16 = mybir.dt.uint16
+U8 = mybir.dt.uint8
+FP8X4 = mybir.dt.float8_e4m3fn_x4
+FP4X4 = mybir.dt.float4_e2m1fn_x4
+MULT = mybir.AluOpType.mult
+ACT = mybir.ActivationFunctionType
+
+P = 128
+PACK = 4
+PASS = P * PACK
+KP = K // PASS
+HP = H // PASS
+MT = S2 // P
+BANK = 512
+CHUNKS = ((0, 256), (256, 128), (384, 128))
+
+
+def tile_list_map_sheet_finder_kernel(
+    tc, tab_words, tab_scales, offs, tab2_words, tab2_scales, offs2, offs3, offs4,
+    w1, b1, page0, wgs, cov, q4_words, q4_scales, cand, out,
+):
+    nc = tc.nc
+    with ExitStack() as ctx:
+        lists = ctx.enter_context(tc.tile_pool(name="lists", bufs=1))
+        keep = ctx.enter_context(tc.tile_pool(name="keep", bufs=1))
+        psum = ctx.enter_context(tc.psum_pool(name="psum", bufs=1))
+
+        def held(shape, dtype, name):
+            return keep.tile(shape, dtype, name=name, align_bytes=64)
+
+        def load_list(src, name):
+            t = lists.tile([P, src.shape[1]], U16, name=name)
+            nc.sync.dma_start(t[:], src)
+            return t
+
+        def load_words(src, name):
+            t = held([P, src.shape[1]], U32, name)
+            nc.sync.dma_start(t[:].bitcast(I32), src.rearrange("p t i -> p (t i)").bitcast(I32))
+            return t
+
+        def load_packed_scales(src, name):
+            passes, width = src.shape[0], src.shape[2]
+            t = held([P, width], U8, name)
+            nc.vector.memset(t[:].bitcast(I32), 0)
+            for q in range(4):
+                nc.gpsimd.dma_start(t[32 * q : 32 * q + 4 * passes, :].bitcast(I32), src[:, 4 * q : 4 * q + 4, :].bitcast(I32))
+            return t
+
+        def gather_bytes(window, offsets, dtype, name):
+            t = held([P, 16 * offsets.shape[1]], dtype, name)
+            nc.vector.tensor_copy(t[:], window[:].indirect(offsets[:]))
+            return t
+
+        w_raw, w_codes, w_scales = {}, {}, {}
+
+        def load_w(a, b):
+            t = keep.tile([P, PACK, PASS], F32, name=f"w_raw{a}{b}", tag="stage", bufs=7, align_bytes=64)
+            nc.sync.dma_start(t[:], w1[PASS * a : PASS * (a + 1), PASS * b : PASS * (b + 1)].rearrange("(p j) c -> p j c", j=PACK))
+            w_raw[a, b] = t
+
+        def quantise_w(a, b, on_vector):
+            g = keep.tile([P, PACK * PASS], BF16, name=f"w_bf{a}{b}", tag="bf", bufs=3, align_bytes=64)
+            dst = g[:].rearrange("p (t m j) -> p m t j", t=PACK, j=PACK)
+            src = w_raw[a, b][:].rearrange("p j (m t) -> p m t j", t=PACK)
+            if on_vector > 0:
+                nc.vector.tensor_copy(dst[:, :on_vector], src[:, :on_vector])
+            if on_vector < P:
+                nc.scalar.copy(dst[:, on_vector:], src[:, on_vector:])
+            w_codes[a, b] = held([P, PASS], U32, f"w_codes{a}{b}")
+            w_scales[a, b] = held([P, PASS], U8, f"w_scales{a}{b}")
+            nc.vector.quantize_mx(out=w_codes[a, b][:].bitcast(FP8X4), scales=w_scales[a, b][:], in_=g[:])
+
+        pages, covs, wg, hs, xs = {}, {}, {}, {}, {}
+
+        def load_page(b, t):
+            pages[b, t] = held([P, T2], F32, f"page{b}{t}")
+            nc.sync.dma_start(pages[b, t][:], page0[PASS * b : PASS * (b + 1), :].rearrange("(p t) c -> p t c", t=PACK)[:, t, :])
+
+        def deal_wgs(rows):
+            ident = held([P, P], F32, "ident")
+            make_identity(nc, ident[:])
+            turned = bank(3, "wgs_turned")
+            for nb in range(S // P):
+                cols = slice(P * nb, P * (nb + 1))
+                nc.tensor.transpose(turned[:, cols], rows[:, cols], ident[:])
+            dealt = keep.tile([P, S // P, PACK, 4, 32], F32, name="wgs_dealt", tag="stage", bufs=7, align_bytes=64)
+            for q in range(4):
+                nc.scalar.copy(dealt[:, :, :, q, :], turned[:].rearrange("p (nb m t) -> p nb t m", t=PACK, m=32))
+            for t in range(PACK):
+                back = bank(4 + t, f"wgs_back{t}")
+                for nb in range(S // P):
+                    nc.tensor.transpose(back[:, P * nb : P * (nb + 1)], dealt[:, nb, t, :, :].rearrange("p q m -> p (q m)"), ident[:])
+                wg[t] = held([P, S], F32, f"wgs{t}")
+                nc.scalar.copy(wg[t][:], back[:])
+
+        def load_cov(b, c):
+            j0, n = CHUNKS[c]
+            covs[b, c] = held([P, PACK, n], F32, f"cov{b}{c}")
+            nc.sync.dma_start(covs[b, c][:], cov[PASS * b : PASS * (b + 1), j0 : j0 + n].rearrange("(p t) j -> p t j", t=PACK))
+
+        def bank(i, name):
+            return psum.tile([P, BANK], F32, name=name, tag=f"bank{i}")
+
+        def first_stage(b):
+            accs = [bank(PACK * b + t, f"h_acc{b}{t}") for t in range(PACK)]
+            for t in range(PACK):
+                for a in range(KP):
+                    cols = slice(P * t, P * (t + 1))
+                    nc.tensor.matmul_mx(
+                        out=accs[t][:], lhsT=w_codes[a, b][:, cols].bitcast(FP8X4), lhsT_scale=w_scales[a, b][:, cols],
+                        rhs=v_words[a][:].bitcast(FP8X4), rhs_scale=v_scales[4 * a :, :],
+                        start=(a == 0), stop=(a == KP - 1),
+                    )
+            for t in range(PACK):
+                hs[b, t] = keep.tile([P, S], F32, name=f"h{b}{t}", tag="h", bufs=5, align_bytes=64)
+                nc.scalar.activation(hs[b, t][:], accs[t][:], ACT.Identity, bias=bias[:, b, t : t + 1])
+
+        def scatter(b, t):
+            nc.vector.tensor_tensor(pages[b, t][:].indirect(list3[:]), hs[b, t][:], wg[t][:], MULT)
+
+        def fetch(b, t, c):
+            j0, n = CHUNKS[c]
+            if t == 0:
+                xs[b, c] = keep.tile([P, PACK, n], F32, name=f"x{b}{c}", tag=f"x_turn{HP * c + b}", align_bytes=64)
+            window = pages[b, t][:].indirect(list4[:, j0 // 16 : (j0 + n) // 16])
+            nc.vector.tensor_tensor(xs[b, c][:, t, :], window, covs[b, c][:, t, :], MULT)
+
+        x_codes, x_scales = {}, {}
+
+        def quantise_x(b, c, on_vector):
+            n = CHUNKS[c][1]
+            g = keep.tile([P, PACK * n], BF16, name=f"x_bf{b}{c}", tag=f"x_turn{HP * c + b + 2}", align_bytes=64)
+            dst = g[:].rearrange("p (c i t) -> p c t i", t=PACK, i=4)
+            src = xs[b, c][:].rearrange("p t (c i) -> p c t i", i=4)
+            if on_vector:
+                nc.vector.tensor_copy(dst, src)
+            else:
+                nc.scalar.copy(dst, src)
+            x_codes[b, c] = held([P, n], U32, f"x_codes{b}{c}")
+            x_scales[b, c] = held([P, n], U8, f"x_scales{b}{c}")
+            nc.vector.quantize_mx(out=x_codes[b, c][:].bitcast(FP8X4), scales=x_scales[b, c][:], in_=g[:])
+
+        e_banks = {}
+
+        def score_pass(c, i, b, with_query, start, stop):
+            j0, n = CHUNKS[c]
+            per_bank = BANK // n
+            for u in range(per_bank):
+                m = per_bank * i + u
+                cols = slice(P * m, P * (m + 1))
+                if with_query:
+                    rhs = q_words[:, b, 2 * j0 : 2 * (j0 + n)].bitcast(FP4X4)
+                    rhs_scale = q_scales[:, b, j0 : j0 + n]
+                else:
+                    rhs = x_codes[b, c][:].bitcast(FP8X4)
+                    rhs_scale = x_scales[b, c][:]
+                nc.tensor.matmul_mx(
+                    out=e_banks[c, i][:, n * u : n * (u + 1)], lhsT=v2_words[b][:, cols].bitcast(FP8X4),
+                    lhsT_scale=v2_scales[b][:, cols], rhs=rhs, rhs_scale=rhs_scale,
+                    start=(start and u == 0), stop=(stop and u == per_bank - 1),
+                )
+
+        def banks_of(c):
+            return range(MT * CHUNKS[c][1] // BANK)
+
+        def finish(c):
+            j0, n = CHUNKS[c]
+            per_bank = BANK // n
+            res = keep.tile([P, MT, n], F32, name=f"res{c}", tag="stage", bufs=7, align_bytes=64)
+            for i in banks_of(c):
+                score_pass(c, i, 1, False, False, True)
+            for i in banks_of(c):
+                ms = range(per_bank * i, per_bank * (i + 1))
+                for u, m in enumerate(ms):
+                    nc.scalar.activation(res[:, m, :], e_banks[c, i][:, n * u : n * (u + 1)], ACT.Tanh, scale=cand_t[:, m : m + 1])
+                nc.sync.dma_start(out.rearrange("(m p) j -> p m j", p=P)[:, ms.start : ms.stop, j0 : j0 + n], res[:, ms.start : ms.stop, :])
+
+        wgs_rows = keep.tile([P, S], F32, name="wgs_rows", tag="x_turn1", align_bytes=64)
+        nc.sync.dma_start(wgs_rows[:], wgs)
+        deal_wgs(wgs_rows)
+        tab2_sc = load_packed_scales(tab2_scales, "tab2_sc")
+        tab_sc = load_packed_scales(tab_scales, "tab_sc")
+        q_scales = held([P, HP, J], U8, "q_scales")
+        nc.vector.memset(q_scales[:].rearrange("p a c -> p (a c)").bitcast(I32), 0)
+        v2_scales1 = held([P, S2], U8, "v2_scales1")
+        nc.vector.memset(v2_scales1[:].bitcast(I32), 0)
+        for q in range(4):
+            nc.gpsimd.dma_start(q_scales[32 * q : 32 * q + 4, :, :].bitcast(I32), q4_scales[:, 4 * q : 4 * q + 4, :].rearrange("a r c -> r a c").bitcast(I32))
+
+        tabw = [load_words(tab_words[0], "tabw0")]
+        list1 = load_list(offs, "list1")
+        load_w(0, 0)
+        list2 = load_list(offs2, "list2")
+        load_w(1, 0)
+        load_w(2, 0)
+        tabw.append(load_words(tab_words[1], "tabw1"))
+        tabw.append(load_words(tab_words[2], "tabw2"))
+        bias = held([P, HP, PACK], F32, "bias")
+        nc.sync.dma_start(bias[:], b1.rearrange("(b p t) -> p b t", p=P, t=PACK))
+        list3 = load_list(offs3, "list3")
+        load_page(0, 0)
+        load_page(0, 1)
+        list4 = load_list(offs4, "list4")
+        load_cov(0, 0)
+        load_page(0, 2)
+        for a in range(KP):
+            load_w(a, 1)
+        tab2w = [load_words(tab2_words[a], f"tab2w{a}") for a in range(HP)]
+        load_page(0, 3)
+        q_words = held([P, HP, 2 * J], U8, "q_words")
+        nc.sync.dma_start(q_words[:].bitcast(I32), q4_words.rearrange("a p c -> p a c").bitcast(I32))
+        load_cov(1, 0)
+        load_page(1, 0)
+        cand_t = held([P, MT], F32, "cand_t")
+        with nc.allow_non_contiguous_dma(reason="one candidate factor a partition"):
+            nc.sync.dma_start(cand_t[:], cand.rearrange("(m p) -> p m", p=P))
+        for t in range(1, PACK):
+            load_page(1, t)
+        for c in range(1, len(CHUNKS)):
+            for b in range(HP):
+                load_cov(b, c)
+
+        v_words = [gather_bytes(tabw[0], list1, U32, "v_words0")]
+        quantise_w(0, 0, P)
+        v2_scales0 = gather_bytes(tab2_sc, list2, U8, "v2_scales0")
+        v_scales = gather_bytes(tab_sc, list1, U8, "v_scales")
+        for q in range(4):
+            nc.gpsimd.dma_start(v2_scales1[32 * q : 32 * q + 4, :].bitcast(I32), v2_scales0[32 * q + 4 : 32 * q + 8, :].bitcast(I32))
+        v2_scales = [v2_scales0, v2_scales1]
+        for a in range(1, KP):
+            quantise_w(a, 0, (0, P // 2)[a - 1])
+            v_words.append(gather_bytes(tabw[a], list1, U32, f"v_words{a}"))
+        first_stage(0)
+        for t in range(PACK - 1):
+            scatter(0, t)
+            fetch(0, t, 0)
+        for a in range(KP):
+            quantise_w(a, 1, 0)
+        first_stage(1)
+        v2_words = [gather_bytes(tab2w[a], list2, U32, f"v2_words{a}") for a in range(HP)]
+        scatter(0, PACK - 1)
+        fetch(0, PACK - 1, 0)
+        quantise_x(0, 0, False)
+
+        first_bank = 0
+        for c in range(len(CHUNKS)):
+            for i in banks_of(c):
+                e_banks[c, i] = bank(first_bank + i, f"e_acc{c}{i}")
+                score_pass(c, i, 0, True, True, False)
+                score_pass(c, i, 1, True, False, False)
+            first_bank += len(banks_of(c))
+        for i in banks_of(0):
+            score_pass(0, i, 0, False, False, False)
+
+        for t in range(PACK):
+            scatter(1, t)
+            fetch(1, t, 0)
+        quantise_x(1, 0, False)
+        finish(0)
+        for c in range(1, len(CHUNKS)):
+            for b in range(HP):
+                for t in range(PACK):
+                    fetch(b, t, c)
+                quantise_x(b, c, b == HP - 1 and c == len(CHUNKS) - 1)
+            for i in banks_of(c):
+                score_pass(c, i, 0, False, False, False)
+            finish(c)

@@ -55,7 +55,7 @@ def tile_list_map_sheet_finder_kernel(
             t = held([P, width], U8, name)
             nc.vector.memset(t[:].bitcast(I32), 0)
             for q in range(4):
-                nc.gpsimd.dma_start(t[32 * q : 32 * q + 4 * passes, :].bitcast(I32), src[:, 4 * q : 4 * q + 4, :].bitcast(I32))
+                (nc.gpsimd, nc.scalar)[q % 2].dma_start(t[32 * q : 32 * q + 4 * passes, :].bitcast(I32), src[:, 4 * q : 4 * q + 4, :].bitcast(I32))
             return t
 
         def gather_bytes(window, offsets, dtype, name):
@@ -105,10 +105,12 @@ def tile_list_map_sheet_finder_kernel(
                 wg[t] = held([P, S], F32, f"wgs{t}")
                 nc.scalar.copy(wg[t][:], back[:])
 
-        def load_cov(b, c):
+        def load_cov(b, c, t0, t1):
             j0, n = CHUNKS[c]
-            covs[b, c] = held([P, PACK, n], F32, f"cov{b}{c}")
-            nc.sync.dma_start(covs[b, c][:], cov[PASS * b : PASS * (b + 1), j0 : j0 + n].rearrange("(p t) j -> p t j", t=PACK))
+            g = held([P, t1 - t0, n], F32, f"cov{b}{c}{t0}")
+            nc.sync.dma_start(g[:], cov[PASS * b : PASS * (b + 1), j0 : j0 + n].rearrange("(p t) j -> p t j", t=PACK)[:, t0:t1, :])
+            for t in range(t0, t1):
+                covs[b, c, t] = g[:, t - t0, :]
 
         def bank(i, name):
             return psum.tile([P, BANK], F32, name=name, tag=f"bank{i}")
@@ -124,7 +126,7 @@ def tile_list_map_sheet_finder_kernel(
                         start=(a == 0), stop=(a == KP - 1),
                     )
             for t in range(PACK):
-                hs[b, t] = keep.tile([P, S], F32, name=f"h{b}{t}", tag="h", bufs=5, align_bytes=64)
+                hs[b, t] = keep.tile([P, S], F32, name=f"h{b}{t}", tag="h", bufs=4, align_bytes=64)
                 nc.scalar.activation(hs[b, t][:], accs[t][:], ACT.Identity, bias=bias[:, b, t : t + 1])
 
         def scatter(b, t):
@@ -135,7 +137,7 @@ def tile_list_map_sheet_finder_kernel(
             if t == 0:
                 xs[b, c] = keep.tile([P, PACK, n], F32, name=f"x{b}{c}", tag=f"x_turn{HP * c + b}", align_bytes=64)
             window = pages[b, t][:].indirect(list4[:, j0 // 16 : (j0 + n) // 16])
-            nc.vector.tensor_tensor(xs[b, c][:, t, :], window, covs[b, c][:, t, :], MULT)
+            nc.vector.tensor_tensor(xs[b, c][:, t, :], window, covs[b, c, t], MULT)
 
         x_codes, x_scales = {}, {}
 
@@ -168,7 +170,7 @@ def tile_list_map_sheet_finder_kernel(
                     rhs_scale = x_scales[b, c][:]
                 nc.tensor.matmul_mx(
                     out=e_banks[c, i][:, n * u : n * (u + 1)], lhsT=v2_words[b][:, cols].bitcast(FP8X4),
-                    lhsT_scale=v2_scales[b][:, cols], rhs=rhs, rhs_scale=rhs_scale,
+                    lhsT_scale=v2_scales[:, b, cols], rhs=rhs, rhs_scale=rhs_scale,
                     start=(start and u == 0), stop=(stop and u == per_bank - 1),
                 )
 
@@ -187,22 +189,25 @@ def tile_list_map_sheet_finder_kernel(
                     nc.scalar.activation(res[:, m, :], e_banks[c, i][:, n * u : n * (u + 1)], ACT.Tanh, scale=cand_t[:, m : m + 1])
                 nc.sync.dma_start(out.rearrange("(m p) j -> p m j", p=P)[:, ms.start : ms.stop, j0 : j0 + n], res[:, ms.start : ms.stop, :])
 
+        tab_sc = load_packed_scales(tab_scales, "tab_sc")
         wgs_rows = keep.tile([P, S], F32, name="wgs_rows", tag="x_turn1", align_bytes=64)
         nc.sync.dma_start(wgs_rows[:], wgs)
         deal_wgs(wgs_rows)
-        tab2_sc = load_packed_scales(tab2_scales, "tab2_sc")
-        tab_sc = load_packed_scales(tab_scales, "tab_sc")
         q_scales = held([P, HP, J], U8, "q_scales")
-        nc.vector.memset(q_scales[:].rearrange("p a c -> p (a c)").bitcast(I32), 0)
-        v2_scales1 = held([P, S2], U8, "v2_scales1")
-        nc.vector.memset(v2_scales1[:].bitcast(I32), 0)
+        nc.gpsimd.memset(q_scales[:].rearrange("p a c -> p (a c)").bitcast(I32), 0)
+        v2_scales = held([P, HP, S2], U8, "v2_scales")
+        nc.gpsimd.memset(v2_scales[:].rearrange("p a c -> p (a c)").bitcast(I32), 0)
+        tab2_sc = held([P, T3], U8, "tab2_sc")
+        nc.vector.memset(tab2_sc[32:64, :].bitcast(I32), 0)
+        nc.vector.memset(tab2_sc[64:128, :].bitcast(I32), 0)
         for q in range(4):
             nc.gpsimd.dma_start(q_scales[32 * q : 32 * q + 4, :, :].bitcast(I32), q4_scales[:, 4 * q : 4 * q + 4, :].rearrange("a r c -> r a c").bitcast(I32))
 
         tabw = [load_words(tab_words[0], "tabw0")]
         list1 = load_list(offs, "list1")
-        load_w(0, 0)
         list2 = load_list(offs2, "list2")
+        nc.sync.dma_start(tab2_sc[0:32, :].bitcast(I32), tab2_scales.rearrange("a q t -> (a q) t").bitcast(I32))
+        load_w(0, 0)
         load_w(1, 0)
         load_w(2, 0)
         tabw.append(load_words(tab_words[1], "tabw1"))
@@ -210,48 +215,57 @@ def tile_list_map_sheet_finder_kernel(
         bias = held([P, HP, PACK], F32, "bias")
         nc.sync.dma_start(bias[:], b1.rearrange("(b p t) -> p b t", p=P, t=PACK))
         list3 = load_list(offs3, "list3")
+        tab2w = [load_words(tab2_words[0], "tab2w0")]
         load_page(0, 0)
         load_page(0, 1)
         list4 = load_list(offs4, "list4")
-        load_cov(0, 0)
+        load_cov(0, 0, 0, 2)
         load_page(0, 2)
         for a in range(KP):
             load_w(a, 1)
-        tab2w = [load_words(tab2_words[a], f"tab2w{a}") for a in range(HP)]
+        tab2w.append(load_words(tab2_words[1], "tab2w1"))
         load_page(0, 3)
+        load_cov(0, 0, 2, 4)
         q_words = held([P, HP, 2 * J], U8, "q_words")
         nc.sync.dma_start(q_words[:].bitcast(I32), q4_words.rearrange("a p c -> p a c").bitcast(I32))
-        load_cov(1, 0)
         load_page(1, 0)
+        load_page(1, 1)
+        load_cov(1, 0, 0, 2)
         cand_t = held([P, MT], F32, "cand_t")
         with nc.allow_non_contiguous_dma(reason="one candidate factor a partition"):
             nc.sync.dma_start(cand_t[:], cand.rearrange("(m p) -> p m", p=P))
-        for t in range(1, PACK):
-            load_page(1, t)
+        load_page(1, 2)
+        load_page(1, 3)
+        load_cov(1, 0, 2, 4)
         for c in range(1, len(CHUNKS)):
             for b in range(HP):
-                load_cov(b, c)
+                load_cov(b, c, 0, PACK)
 
         v_words = [gather_bytes(tabw[0], list1, U32, "v_words0")]
+        v2_rows = gather_bytes(tab2_sc, list2, U8, "v2_rows")
         quantise_w(0, 0, P)
-        v2_scales0 = gather_bytes(tab2_sc, list2, U8, "v2_scales0")
         v_scales = gather_bytes(tab_sc, list1, U8, "v_scales")
-        for q in range(4):
-            nc.gpsimd.dma_start(v2_scales1[32 * q : 32 * q + 4, :].bitcast(I32), v2_scales0[32 * q + 4 : 32 * q + 8, :].bitcast(I32))
-        v2_scales = [v2_scales0, v2_scales1]
+        for a in range(HP):
+            for q in range(4):
+                rows = slice(16 * a + 4 * q, 16 * a + 4 * q + 4)
+                nc.gpsimd.dma_start(v2_scales[32 * q : 32 * q + 4, a, :].bitcast(I32), v2_rows[rows, :].bitcast(I32))
         for a in range(1, KP):
             quantise_w(a, 0, (0, P // 2)[a - 1])
             v_words.append(gather_bytes(tabw[a], list1, U32, f"v_words{a}"))
         first_stage(0)
-        for t in range(PACK - 1):
-            scatter(0, t)
-            fetch(0, t, 0)
+        v2_words = [gather_bytes(tab2w[0], list2, U32, "v2_words0")]
+        scatter(0, 0)
+        scatter(0, 1)
+        fetch(0, 0, 0)
+        fetch(0, 1, 0)
+        scatter(0, 2)
         for a in range(KP):
             quantise_w(a, 1, 0)
         first_stage(1)
-        v2_words = [gather_bytes(tab2w[a], list2, U32, f"v2_words{a}") for a in range(HP)]
-        scatter(0, PACK - 1)
-        fetch(0, PACK - 1, 0)
+        v2_words.append(gather_bytes(tab2w[1], list2, U32, "v2_words1"))
+        scatter(0, 3)
+        fetch(0, 2, 0)
+        fetch(0, 3, 0)
         quantise_x(0, 0, False)
 
         first_bank = 0
@@ -264,9 +278,11 @@ def tile_list_map_sheet_finder_kernel(
         for i in banks_of(0):
             score_pass(0, i, 0, False, False, False)
 
-        for t in range(PACK):
+        for t in range(0, PACK, 2):
             scatter(1, t)
+            scatter(1, t + 1)
             fetch(1, t, 0)
+            fetch(1, t + 1, 0)
         quantise_x(1, 0, False)
         finish(0)
         for c in range(1, len(CHUNKS)):

@@ -25,6 +25,8 @@ HP = H // PASS
 MT = S2 // P
 BANK = 512
 CHUNKS = ((0, 256), (256, 128), (384, 128))
+X_TAG = {(0, 0): "x_first", (1, 0): "x_a", (0, 1): "x_b", (1, 1): "x_c", (0, 2): "x_a", (1, 2): "x_c"}
+H_TAG = {(1, 2): "x_c", (1, 3): "x_b"}
 
 
 def tile_list_map_sheet_finder_kernel(
@@ -126,7 +128,10 @@ def tile_list_map_sheet_finder_kernel(
                         start=(a == 0), stop=(a == KP - 1),
                     )
             for t in range(PACK):
-                hs[b, t] = keep.tile([P, S], F32, name=f"h{b}{t}", tag="h", bufs=4, align_bytes=64)
+                if (b, t) in H_TAG:
+                    hs[b, t] = keep.tile([P, S], F32, name=f"h{b}{t}", tag=H_TAG[b, t], align_bytes=64)
+                else:
+                    hs[b, t] = keep.tile([P, S], F32, name=f"h{b}{t}", tag="h", bufs=4, align_bytes=64)
                 nc.scalar.activation(hs[b, t][:], accs[t][:], ACT.Identity, bias=bias[:, b, t : t + 1])
 
         def scatter(b, t):
@@ -135,7 +140,7 @@ def tile_list_map_sheet_finder_kernel(
         def fetch(b, t, c):
             j0, n = CHUNKS[c]
             if t == 0:
-                xs[b, c] = keep.tile([P, PACK, n], F32, name=f"x{b}{c}", tag=f"x_turn{HP * c + b}", align_bytes=64)
+                xs[b, c] = keep.tile([P, PACK, n], F32, name=f"x{b}{c}", tag=X_TAG[b, c], align_bytes=64)
             window = pages[b, t][:].indirect(list4[:, j0 // 16 : (j0 + n) // 16])
             nc.vector.tensor_tensor(xs[b, c][:, t, :], window, covs[b, c, t], MULT)
 
@@ -143,7 +148,7 @@ def tile_list_map_sheet_finder_kernel(
 
         def quantise_x(b, c, on_vector):
             n = CHUNKS[c][1]
-            g = keep.tile([P, PACK * n], BF16, name=f"x_bf{b}{c}", tag=f"x_turn{HP * c + b + 2}", align_bytes=64)
+            g = keep.tile([P, PACK * n], BF16, name=f"x_bf{b}{c}", tag="bf", bufs=3, align_bytes=64)
             dst = g[:].rearrange("p (c i t) -> p c t i", t=PACK, i=4)
             src = xs[b, c][:].rearrange("p t (c i) -> p c t i", i=4)
             if on_vector:
@@ -190,7 +195,7 @@ def tile_list_map_sheet_finder_kernel(
                 nc.sync.dma_start(out.rearrange("(m p) j -> p m j", p=P)[:, ms.start : ms.stop, j0 : j0 + n], res[:, ms.start : ms.stop, :])
 
         tab_sc = load_packed_scales(tab_scales, "tab_sc")
-        wgs_rows = keep.tile([P, S], F32, name="wgs_rows", tag="x_turn1", align_bytes=64)
+        wgs_rows = keep.tile([P, S], F32, name="wgs_rows", tag="x_first", align_bytes=64)
         nc.sync.dma_start(wgs_rows[:], wgs)
         deal_wgs(wgs_rows)
         q_scales = held([P, HP, J], U8, "q_scales")
@@ -200,13 +205,12 @@ def tile_list_map_sheet_finder_kernel(
         tab2_sc = held([P, T3], U8, "tab2_sc")
         nc.vector.memset(tab2_sc[32:64, :].bitcast(I32), 0)
         nc.vector.memset(tab2_sc[64:128, :].bitcast(I32), 0)
-        for q in range(4):
-            nc.gpsimd.dma_start(q_scales[32 * q : 32 * q + 4, :, :].bitcast(I32), q4_scales[:, 4 * q : 4 * q + 4, :].rearrange("a r c -> r a c").bitcast(I32))
 
         tabw = [load_words(tab_words[0], "tabw0")]
         list1 = load_list(offs, "list1")
         list2 = load_list(offs2, "list2")
         nc.sync.dma_start(tab2_sc[0:32, :].bitcast(I32), tab2_scales.rearrange("a q t -> (a q) t").bitcast(I32))
+        v2_rows = gather_bytes(tab2_sc, list2, U8, "v2_rows")
         load_w(0, 0)
         load_w(1, 0)
         load_w(2, 0)
@@ -220,16 +224,23 @@ def tile_list_map_sheet_finder_kernel(
         load_page(0, 1)
         list4 = load_list(offs4, "list4")
         load_cov(0, 0, 0, 2)
+        load_w(0, 1)
+        load_w(1, 1)
         load_page(0, 2)
-        for a in range(KP):
-            load_w(a, 1)
+        load_w(2, 1)
         tab2w.append(load_words(tab2_words[1], "tab2w1"))
         load_page(0, 3)
         load_cov(0, 0, 2, 4)
-        q_words = held([P, HP, 2 * J], U8, "q_words")
-        nc.sync.dma_start(q_words[:].bitcast(I32), q4_words.rearrange("a p c -> p a c").bitcast(I32))
         load_page(1, 0)
         load_page(1, 1)
+        q_words = held([P, HP, 2 * J], U8, "q_words")
+        nc.sync.dma_start(q_words[:].bitcast(I32), q4_words.rearrange("a p c -> p a c").bitcast(I32))
+        for q in range(4):
+            nc.sync.dma_start(q_scales[32 * q : 32 * q + 4, :, :].bitcast(I32), q4_scales[:, 4 * q : 4 * q + 4, :].rearrange("a r c -> r a c").bitcast(I32))
+        for a in range(HP):
+            for q in range(4):
+                rows = slice(16 * a + 4 * q, 16 * a + 4 * q + 4)
+                nc.sync.dma_start(v2_scales[32 * q : 32 * q + 4, a, :].bitcast(I32), v2_rows[rows, :].bitcast(I32))
         load_cov(1, 0, 0, 2)
         cand_t = held([P, MT], F32, "cand_t")
         with nc.allow_non_contiguous_dma(reason="one candidate factor a partition"):
@@ -242,13 +253,8 @@ def tile_list_map_sheet_finder_kernel(
                 load_cov(b, c, 0, PACK)
 
         v_words = [gather_bytes(tabw[0], list1, U32, "v_words0")]
-        v2_rows = gather_bytes(tab2_sc, list2, U8, "v2_rows")
         quantise_w(0, 0, P)
         v_scales = gather_bytes(tab_sc, list1, U8, "v_scales")
-        for a in range(HP):
-            for q in range(4):
-                rows = slice(16 * a + 4 * q, 16 * a + 4 * q + 4)
-                nc.gpsimd.dma_start(v2_scales[32 * q : 32 * q + 4, a, :].bitcast(I32), v2_rows[rows, :].bitcast(I32))
         for a in range(1, KP):
             quantise_w(a, 0, (0, P // 2)[a - 1])
             v_words.append(gather_bytes(tabw[a], list1, U32, f"v_words{a}"))
@@ -289,7 +295,7 @@ def tile_list_map_sheet_finder_kernel(
             for b in range(HP):
                 for t in range(PACK):
                     fetch(b, t, c)
-                quantise_x(b, c, b == HP - 1 and c == len(CHUNKS) - 1)
+                quantise_x(b, c, c == len(CHUNKS) - 1)
             for i in banks_of(c):
                 score_pass(c, i, 0, False, False, False)
             finish(c)

from contextlib import ExitStack

import concourse.mybir as mybir
from concourse.masks import make_identity

K, H, T, S, T2, J, T3, S2 = 1536, 1024, 2048, 512, 1024, 512, 2048, 1024
FLOPS = 2 * K * H * S + 2 * 2 * H * S2 * J

F32 = mybir.dt.float32
BF16 = mybir.dt.bfloat16
I32 = mybir.dt.int32
U32 = mybir.dt.uint32
U16 = mybir.dt.uint16
U8 = mybir.dt.uint8
FP8X4 = mybir.dt.float8_e4m3fn_x4
FP4X4 = mybir.dt.float4_e2m1fn_x4
MULT = mybir.AluOpType.mult
ACT = mybir.ActivationFunctionType

P = 128
PACK = 4
PASS = P * PACK
KP = K // PASS
HP = H // PASS
MT = S2 // P
BANK = 512
CHUNKS = ((0, 256), (256, 128), (384, 128))
X_TAG = {(0, 0): "x_first", (1, 0): "x_a", (0, 1): "x_b", (1, 1): "x_c", (0, 2): "x_a", (1, 2): "x_c"}
H_TAG = {(1, 2): "x_c", (1, 3): "x_b"}


def tile_list_map_sheet_finder_kernel(
    tc, tab_words, tab_scales, offs, tab2_words, tab2_scales, offs2, offs3, offs4,
    w1, b1, page0, wgs, cov, q4_words, q4_scales, cand, out,
):
    nc = tc.nc
    with ExitStack() as ctx:
        lists = ctx.enter_context(tc.tile_pool(name="lists", bufs=1))
        keep = ctx.enter_context(tc.tile_pool(name="keep", bufs=1))
        psum = ctx.enter_context(tc.psum_pool(name="psum", bufs=1))

        def held(shape, dtype, name):
            return keep.tile(shape, dtype, name=name, align_bytes=64)

        def load_list(src, name):
            t = lists.tile([P, src.shape[1]], U16, name=name)
            nc.sync.dma_start(t[:], src)
            return t

        def load_words(src, name):
            t = held([P, src.shape[1]], U32, name)
            nc.sync.dma_start(t[:].bitcast(I32), src.rearrange("p t i -> p (t i)").bitcast(I32))
            return t

        def load_packed_scales(src, name):
            passes, width = src.shape[0], src.shape[2]
            t = held([P, width], U8, name)
            nc.vector.memset(t[:].bitcast(I32), 0)
            for q in range(4):
                (nc.gpsimd, nc.scalar)[q % 2].dma_start(t[32 * q : 32 * q + 4 * passes, :].bitcast(I32), src[:, 4 * q : 4 * q + 4, :].bitcast(I32))
            return t

        def gather_bytes(window, offsets, dtype, name):
            t = held([P, 16 * offsets.shape[1]], dtype, name)
            nc.vector.tensor_copy(t[:], window[:].indirect(offsets[:]))
            return t

        w_raw, w_codes, w_scales = {}, {}, {}

        def load_w(a, b):
            t = keep.tile([P, PACK, PASS], F32, name=f"w_raw{a}{b}", tag="stage", bufs=7, align_bytes=64)
            nc.sync.dma_start(t[:], w1[PASS * a : PASS * (a + 1), PASS * b : PASS * (b + 1)].rearrange("(p j) c -> p j c", j=PACK))
            w_raw[a, b] = t

        def quantise_w(a, b, on_vector):
            g = keep.tile([P, PACK * PASS], BF16, name=f"w_bf{a}{b}", tag="bf", bufs=3, align_bytes=64)
            dst = g[:].rearrange("p (t m j) -> p m t j", t=PACK, j=PACK)
            src = w_raw[a, b][:].rearrange("p j (m t) -> p m t j", t=PACK)
            if on_vector > 0:
                nc.vector.tensor_copy(dst[:, :on_vector], src[:, :on_vector])
            if on_vector < P:
                nc.scalar.copy(dst[:, on_vector:], src[:, on_vector:])
            w_codes[a, b] = held([P, PASS], U32, f"w_codes{a}{b}")
            w_scales[a, b] = held([P, PASS], U8, f"w_scales{a}{b}")
            nc.vector.quantize_mx(out=w_codes[a, b][:].bitcast(FP8X4), scales=w_scales[a, b][:], in_=g[:])

        pages, covs, wg, hs, xs = {}, {}, {}, {}, {}

        def load_page(b, t):
            pages[b, t] = held([P, T2], F32, f"page{b}{t}")
            nc.sync.dma_start(pages[b, t][:], page0[PASS * b : PASS * (b + 1), :].rearrange("(p t) c -> p t c", t=PACK)[:, t, :])

        def deal_wgs(rows):
            ident = held([P, P], F32, "ident")
            make_identity(nc, ident[:])
            turned = bank(3, "wgs_turned")
            for nb in range(S // P):
                cols = slice(P * nb, P * (nb + 1))
                nc.tensor.transpose(turned[:, cols], rows[:, cols], ident[:])
            dealt = keep.tile([P, S // P, PACK, 4, 32], F32, name="wgs_dealt", tag="stage", bufs=7, align_bytes=64)
            for q in range(4):
                nc.scalar.copy(dealt[:, :, :, q, :], turned[:].rearrange("p (nb m t) -> p nb t m", t=PACK, m=32))
            for t in range(PACK):
                back = bank(4 + t, f"wgs_back{t}")
                for nb in range(S // P):
                    nc.tensor.transpose(back[:, P * nb : P * (nb + 1)], dealt[:, nb, t, :, :].rearrange("p q m -> p (q m)"), ident[:])
                wg[t] = held([P, S], F32, f"wgs{t}")
                nc.scalar.copy(wg[t][:], back[:])

        def load_cov(b, c, t0, t1):
            j0, n = CHUNKS[c]
            g = held([P, t1 - t0, n], F32, f"cov{b}{c}{t0}")
            nc.sync.dma_start(g[:], cov[PASS * b : PASS * (b + 1), j0 : j0 + n].rearrange("(p t) j -> p t j", t=PACK)[:, t0:t1, :])
            for t in range(t0, t1):
                covs[b, c, t] = g[:, t - t0, :]

        def bank(i, name):
            return psum.tile([P, BANK], F32, name=name, tag=f"bank{i}")

        def first_stage(b):
            accs = [bank(PACK * b + t, f"h_acc{b}{t}") for t in range(PACK)]
            for t in range(PACK):
                for a in range(KP):
                    cols = slice(P * t, P * (t + 1))
                    nc.tensor.matmul_mx(
                        out=accs[t][:], lhsT=w_codes[a, b][:, cols].bitcast(FP8X4), lhsT_scale=w_scales[a, b][:, cols],
                        rhs=v_words[a][:].bitcast(FP8X4), rhs_scale=v_scales[4 * a :, :],
                        start=(a == 0), stop=(a == KP - 1),
                    )
            for t in range(PACK):
                if (b, t) in H_TAG:
                    hs[b, t] = keep.tile([P, S], F32, name=f"h{b}{t}", tag=H_TAG[b, t], align_bytes=64)
                else:
                    hs[b, t] = keep.tile([P, S], F32, name=f"h{b}{t}", tag="h", bufs=4, align_bytes=64)
                nc.scalar.activation(hs[b, t][:], accs[t][:], ACT.Identity, bias=bias[:, b, t : t + 1])

        def scatter(b, t):
            nc.vector.tensor_tensor(pages[b, t][:].indirect(list3[:]), hs[b, t][:], wg[t][:], MULT)

        def fetch(b, t, c):
            j0, n = CHUNKS[c]
            if t == 0:
                xs[b, c] = keep.tile([P, PACK, n], F32, name=f"x{b}{c}", tag=X_TAG[b, c], align_bytes=64)
            window = pages[b, t][:].indirect(list4[:, j0 // 16 : (j0 + n) // 16])
            nc.vector.tensor_tensor(xs[b, c][:, t, :], window, covs[b, c, t], MULT)

        x_codes, x_scales = {}, {}

        def quantise_x(b, c, on_vector):
            n = CHUNKS[c][1]
            g = keep.tile([P, PACK * n], BF16, name=f"x_bf{b}{c}", tag="bf", bufs=3, align_bytes=64)
            dst = g[:].rearrange("p (c i t) -> p c t i", t=PACK, i=4)
            src = xs[b, c][:].rearrange("p t (c i) -> p c t i", i=4)
            if on_vector:
                nc.vector.tensor_copy(dst, src)
            else:
                nc.scalar.copy(dst, src)
            x_codes[b, c] = held([P, n], U32, f"x_codes{b}{c}")
            x_scales[b, c] = held([P, n], U8, f"x_scales{b}{c}")
            nc.vector.quantize_mx(out=x_codes[b, c][:].bitcast(FP8X4), scales=x_scales[b, c][:], in_=g[:])

        e_banks = {}

        def score_pass(c, i, b, with_query, start, stop):
            j0, n = CHUNKS[c]
            per_bank = BANK // n
            for u in range(per_bank):
                m = per_bank * i + u
                cols = slice(P * m, P * (m + 1))
                if with_query:
                    rhs = q_words[:, b, 2 * j0 : 2 * (j0 + n)].bitcast(FP4X4)
                    rhs_scale = q_scales[:, b, j0 : j0 + n]
                else:
                    rhs = x_codes[b, c][:].bitcast(FP8X4)
                    rhs_scale = x_scales[b, c][:]
                nc.tensor.matmul_mx(
                    out=e_banks[c, i][:, n * u : n * (u + 1)], lhsT=v2_words[b][:, cols].bitcast(FP8X4),
                    lhsT_scale=v2_scales[:, b, cols], rhs=rhs, rhs_scale=rhs_scale,
                    start=(start and u == 0), stop=(stop and u == per_bank - 1),
                )

        def banks_of(c):
            return range(MT * CHUNKS[c][1] // BANK)

        def finish(c):
            j0, n = CHUNKS[c]
            per_bank = BANK // n
            res = keep.tile([P, MT, n], F32, name=f"res{c}", tag="stage", bufs=7, align_bytes=64)
            for i in banks_of(c):
                score_pass(c, i, 1, False, False, True)
            for i in banks_of(c):
                ms = range(per_bank * i, per_bank * (i + 1))
                for u, m in enumerate(ms):
                    nc.scalar.activation(res[:, m, :], e_banks[c, i][:, n * u : n * (u + 1)], ACT.Tanh, scale=cand_t[:, m : m + 1])
                nc.sync.dma_start(out.rearrange("(m p) j -> p m j", p=P)[:, ms.start : ms.stop, j0 : j0 + n], res[:, ms.start : ms.stop, :])

        tab_sc = load_packed_scales(tab_scales, "tab_sc")
        wgs_rows = keep.tile([P, S], F32, name="wgs_rows", tag="x_first", align_bytes=64)
        nc.sync.dma_start(wgs_rows[:], wgs)
        deal_wgs(wgs_rows)
        q_scales = held([P, HP, J], U8, "q_scales")
        nc.gpsimd.memset(q_scales[:].rearrange("p a c -> p (a c)").bitcast(I32), 0)
        v2_scales = held([P, HP, S2], U8, "v2_scales")
        nc.gpsimd.memset(v2_scales[:].rearrange("p a c -> p (a c)").bitcast(I32), 0)
        tab2_sc = held([P, T3], U8, "tab2_sc")
        nc.vector.memset(tab2_sc[32:64, :].bitcast(I32), 0)
        nc.vector.memset(tab2_sc[64:128, :].bitcast(I32), 0)

        tabw = [load_words(tab_words[0], "tabw0")]
        list1 = load_list(offs, "list1")
        list2 = load_list(offs2, "list2")
        nc.sync.dma_start(tab2_sc[0:32, :].bitcast(I32), tab2_scales.rearrange("a q t -> (a q) t").bitcast(I32))
        v2_rows = gather_bytes(tab2_sc, list2, U8, "v2_rows")
        load_w(0, 0)
        load_w(1, 0)
        load_w(2, 0)
        tabw.append(load_words(tab_words[1], "tabw1"))
        tabw.append(load_words(tab_words[2], "tabw2"))
        bias = held([P, HP, PACK], F32, "bias")
        nc.sync.dma_start(bias[:], b1.rearrange("(b p t) -> p b t", p=P, t=PACK))
        list3 = load_list(offs3, "list3")
        tab2w = [load_words(tab2_words[0], "tab2w0")]
        load_page(0, 0)
        load_page(0, 1)
        list4 = load_list(offs4, "list4")
        load_cov(0, 0, 0, 2)
        load_w(0, 1)
        load_w(1, 1)
        load_page(0, 2)
        load_w(2, 1)
        tab2w.append(load_words(tab2_words[1], "tab2w1"))
        load_page(0, 3)
        load_cov(0, 0, 2, 4)
        load_page(1, 0)
        load_page(1, 1)
        q_words = held([P, HP, 2 * J], U8, "q_words")
        nc.sync.dma_start(q_words[:].bitcast(I32), q4_words.rearrange("a p c -> p a c").bitcast(I32))
        for q in range(4):
            nc.sync.dma_start(q_scales[32 * q : 32 * q + 4, :, :].bitcast(I32), q4_scales[:, 4 * q : 4 * q + 4, :].rearrange("a r c -> r a c").bitcast(I32))
        for a in range(HP):
            for q in range(4):
                rows = slice(16 * a + 4 * q, 16 * a + 4 * q + 4)
                nc.sync.dma_start(v2_scales[32 * q : 32 * q + 4, a, :].bitcast(I32), v2_rows[rows, :].bitcast(I32))
        load_cov(1, 0, 0, 2)
        cand_t = held([P, MT], F32, "cand_t")
        with nc.allow_non_contiguous_dma(reason="one candidate factor a partition"):
            nc.sync.dma_start(cand_t[:], cand.rearrange("(m p) -> p m", p=P))
        load_page(1, 2)
        load_page(1, 3)
        load_cov(1, 0, 2, 4)
        for c in range(1, len(CHUNKS)):
            for b in range(HP):
                load_cov(b, c, 0, PACK)

        v_words = [gather_bytes(tabw[0], list1, U32, "v_words0")]
        quantise_w(0, 0, P)
        v_scales = gather_bytes(tab_sc, list1, U8, "v_scales")
        for a in range(1, KP):
            quantise_w(a, 0, (0, P // 2)[a - 1])
            v_words.append(gather_bytes(tabw[a], list1, U32, f"v_words{a}"))
        first_stage(0)
        v2_words = [gather_bytes(tab2w[0], list2, U32, "v2_words0")]
        scatter(0, 0)
        scatter(0, 1)
        fetch(0, 0, 0)
        fetch(0, 1, 0)
        scatter(0, 2)
        for a in range(KP):
            quantise_w(a, 1, 0)
        first_stage(1)
        v2_words.append(gather_bytes(tab2w[1], list2, U32, "v2_words1"))
        scatter(0, 3)
        fetch(0, 2, 0)
        fetch(0, 3, 0)
        quantise_x(0, 0, False)

        first_bank = 0
        for c in range(len(CHUNKS)):
            for i in banks_of(c):
                e_banks[c, i] = bank(first_bank + i, f"e_acc{c}{i}")
                score_pass(c, i, 0, True, True, False)
                score_pass(c, i, 1, True, False, False)
            first_bank += len(banks_of(c))
        for i in banks_of(0):
            score_pass(0, i, 0, False, False, False)

        for t in range(0, PACK, 2):
            scatter(1, t)
            scatter(1, t + 1)
            fetch(1, t, 0)
            fetch(1, t + 1, 0)
        quantise_x(1, 0, False)
        finish(0)
        for c in range(1, len(CHUNKS)):
            for b in range(HP):
                for t in range(PACK):
                    fetch(b, t, c)
                quantise_x(b, c, c == len(CHUNKS) - 1)
            for i in banks_of(c):
                score_pass(c, i, 0, False, False, False)
            finish(c)
